import numpy as np
import ml_dtypes


def mxq(x, axis, fmt="e4m3"):
    dtype, down = {"e4m3": (ml_dtypes.float8_e4m3fn, 7), "e5m2": (ml_dtypes.float8_e5m2, 14)}[fmt]
    v = np.moveaxis(np.asarray(x, np.float32).astype(ml_dtypes.bfloat16).astype(np.float64), axis, -1)
    blocks = v.reshape(v.shape[:-1] + (-1, 32))
    amax = np.abs(blocks).max(-1, keepdims=True)
    byte = np.maximum(np.where(amax > 0, np.frexp(amax)[1] - 1 + 127, 0) - down, 1)
    scale = np.exp2(byte - 127.0)
    codes = (blocks / scale).astype(np.float32).astype(dtype).astype(np.float64)
    return np.moveaxis((codes * scale).reshape(v.shape), -1, axis)


WIDE = False


def mx_kscale(k):
    if not WIDE:
        return np.ones(k)
    levels = np.array([10, -10, 5, -5, 0])
    if k % 512:
        return np.exp2(np.random.permutation(np.resize(levels, k // 32))).repeat(32)
    a = np.empty((k // 512, 16))
    for p in range(k // 512):
        a[p, :8] = np.random.permutation(np.resize(levels, 8))
        for g in range(8):
            far = levels[np.abs(levels - a[p, g]) >= 10]
            a[p, g + 8] = far[np.random.randint(len(far))]
    return np.exp2(a.ravel()).repeat(32)


def f64(x):
    return np.asarray(x).astype(np.float64)


def striped(idx):
    return np.tile(idx.reshape(-1, 16).T, (8, 1)).astype(np.uint16)


def unstriped(offs):
    return offs[:16].T.reshape(-1).astype(np.int64)


def pack_weight(w):
    k, n = w.shape
    w = f64(np.asarray(w, np.float32).astype(ml_dtypes.bfloat16)).reshape(k // 32, 32, n)
    amax = np.abs(w).max(1)
    byte = np.clip(np.where(amax > 0, np.frexp(amax)[1] - 1 + 127 - 7, 1), 1, 254)
    scaled = (w * np.exp2(127.0 - byte)[:, None, :]).reshape(k, n).astype(np.float32)
    words = np.ascontiguousarray(scaled.reshape(k // 512, 128, 4, n).transpose(0, 1, 3, 2)).astype(ml_dtypes.float8_e4m3fn).view(np.uint8)
    return words, np.ascontiguousarray(byte.astype(np.uint8).reshape(k // 512, 16, n))


def unpack_weight(words, scales):
    g, p, n, _ = words.shape
    vals = np.ascontiguousarray(words).view(ml_dtypes.float8_e4m3fn).astype(np.float64) * np.repeat(np.exp2(scales.astype(np.float64) - 127.0), 8, axis=1)[..., None]
    return vals.transpose(0, 1, 3, 2).reshape(g * 512, n)


K, T, S, N = 512, 1024, 512, 128
P = 2 ** 7


def setup_inputs():
    n = np.random.standard_normal
    s = mx_kscale(K)[:, None]
    packed_xT = pack_weight(n((K, T)) * s)
    return {
        "x_words": packed_xT[0],
        "x_scales": packed_xT[1],
        "mean": np.tile(0.3 * np.random.standard_normal(T), (P, 1)).astype(np.float32),
        "inv": np.tile(np.random.uniform(0.5, 2.0, T), (P, 1)).astype(np.float32),
        "gsum": n((N, 1)).astype(np.float32),
        "b": (0.3 * n((N, 1))).astype(np.float32),
        "w1": (n((K, N)) / np.sqrt(K) / s).astype(np.float32),
        "offs": striped(np.random.permutation(T)[:S]),
    }


def reference(x_words, x_scales, mean, inv, gsum, b, w1, offs):
    xq = unpack_weight(x_words, x_scales)[:, unstriped(offs)]
    y = mxq(f64(w1), 0, "e4m3").T @ xq
    mg = f64(mean)[:1][:, unstriped(offs)]
    ig = f64(inv)[:1][:, unstriped(offs)]
    return (y - (f64(gsum) * mg)) * ig + f64(b)

@@ -1,0 +1,146 @@
+from contextlib import ExitStack
+
+import concourse.mybir as mybir
+from concourse.masks import make_identity
+
+K, T, S, N = 512, 1024, 512, 128
+FLOPS = 2 * K * S * N
+
+F32 = mybir.dt.float32
+BF16 = mybir.dt.bfloat16
+I32 = mybir.dt.int32
+U32 = mybir.dt.uint32
+U16 = mybir.dt.uint16
+U8 = mybir.dt.uint8
+FP8X4 = mybir.dt.float8_e4m3fn_x4
+MULT = mybir.AluOpType.mult
+ADD = mybir.AluOpType.add
+COPY = mybir.ActivationFunctionType.Copy
+IDENTITY = mybir.ActivationFunctionType.Identity
+
+P = 128
+PACK = 4
+HALF = S // 2
+BLOCKS = HALF // P
+MEAN_ROW, INV_ROW = P - 2, P - 1
+PIECES = [(0, 256), (256, 384), (384, 512)]
+ACC_TAG = ["acc0", "acc1", "turned0"]
+
+
+def tile_picked_lnfold_none_p_kernel(
+    tc, x_words, x_scales, mean, inv, gsum, b, w1, offs, out
+):
+    nc = tc.nc
+    with ExitStack() as ctx:
+        sb = ctx.enter_context(tc.tile_pool(name="sb", bufs=1))
+        shared = ctx.enter_context(tc.tile_pool(name="shared", bufs=1))
+        ps = ctx.enter_context(tc.psum_pool(name="ps", bufs=1))
+
+        offsets = sb.tile([P, S // 16], U16, name="offsets")
+        nc.sync.dma_start(offsets[:], offs)
+
+        def entries(h):
+            return offsets[:, h * HALF // 16 : (h + 1) * HALF // 16]
+
+        stat_table = shared.tile([P, T], F32, name="stat_table", align_bytes=64, offset=0)
+        nc.sync.dma_start(out=stat_table[MEAN_ROW : MEAN_ROW + 1, :], in_=mean[0:1, :])
+        nc.sync.dma_start(out=stat_table[INV_ROW : INV_ROW + 1, :], in_=inv[0:1, :])
+        nc.vector.memset(stat_table[0:MEAN_ROW, :], 0.0)
+
+        word_table = sb.tile([P, T], I32, name="word_table", align_bytes=64)
+        nc.sync.dma_start(out=word_table[:], in_=x_words[0].rearrange("p n t -> p (n t)").bitcast(I32))
+
+        scale_table = sb.tile([P, T], U8, name="scale_table", align_bytes=64)
+        nc.vector.memset(scale_table[:].bitcast(I32), 0)
+        w_raw = sb.tile([P, PACK, N], F32, name="w_raw", align_bytes=64)
+        nc.sync.dma_start(out=w_raw[:], in_=w1.rearrange("(p j) n -> p j n", j=PACK))
+        for q in range(4):
+            nc.sync.dma_start(
+                out=scale_table[32 * q : 32 * q + 4, :].bitcast(I32),
+                in_=x_scales[0, 4 * q : 4 * q + 4, :].bitcast(I32),
+            )
+        identity = sb.tile([P, P], F32, name="identity", align_bytes=64)
+        nc.vector.memset(identity[:], 0.0)
+        make_identity(nc, identity[:], nomemset=True)
+
+        gsum_col = sb.tile([P, 1], F32, name="gsum_col")
+        bias_col = sb.tile([P, 1], F32, name="bias_col")
+        with nc.allow_non_contiguous_dma(reason="one value a partition"):
+            nc.scalar.dma_start(out=gsum_col[:], in_=gsum)
+            nc.scalar.dma_start(out=bias_col[:], in_=b)
+
+        w_grouped = sb.tile([P, N, PACK], BF16, name="w_grouped", align_bytes=64)
+        nc.scalar.activation(w_grouped[:], w_raw[:].rearrange("p j n -> p n j"), COPY)
+
+        neg_gsum = sb.tile([P, 1], F32, name="neg_gsum")
+        nc.scalar.activation(neg_gsum[:], gsum_col[:], COPY, scale=-1.0)
+
+        inv_rows, shift_rows = [], []
+        for h in range(2):
+            picked = sb.tile([P, HALF], F32, name=f"picked{h}", align_bytes=64)
+            nc.vector.tensor_copy(picked[:], stat_table[:].indirect(entries(h)))
+            turned = ps.tile([P, BLOCKS, P], F32, name=f"turned{h}")
+            for c in range(BLOCKS):
+                nc.tensor.transpose(turned[:, c, :], picked[:, c * P : (c + 1) * P], identity[:])
+            cols = sb.tile([P, BLOCKS, 2], F32, name=f"cols{h}")
+            nc.scalar.copy(out=cols[:], in_=turned[:, :, MEAN_ROW:P])
+            prod = sb.tile([P, BLOCKS], F32, name=f"prod{h}")
+            for c in range(BLOCKS):
+                nc.scalar.activation(
+                    prod[:, c : c + 1], cols[:, c, 0:1], COPY,
+                    scale=cols[:, c, 1:2],
+                )
+            inv_ps = ps.tile([P, HALF], F32, name=f"inv_ps{h}")
+            prod_ps = ps.tile([P, HALF], F32, name=f"prod_ps{h}")
+            for c in range(BLOCKS):
+                nc.tensor.transpose(
+                    inv_ps[:, c * P : (c + 1) * P],
+                    cols[:, c, 1:2].to_broadcast([P, P]),
+                    identity[:],
+                )
+            for c in range(BLOCKS):
+                nc.tensor.transpose(
+                    prod_ps[:, c * P : (c + 1) * P], prod[:, c : c + 1].to_broadcast([P, P]), identity[:]
+                )
+            inv_row = sb.tile([P, HALF], F32, name=f"inv_row{h}", align_bytes=64)
+            nc.scalar.copy(out=inv_row[:], in_=inv_ps[:])
+            shift_row = sb.tile([P, HALF], F32, name=f"shift_row{h}", align_bytes=64)
+            nc.scalar.activation(shift_row[:], prod_ps[:], IDENTITY, bias=bias_col[:], scale=neg_gsum[:])
+            inv_rows.append(inv_row)
+            shift_rows.append(shift_row)
+
+        x_codes = sb.tile([P, S], U32, name="x_codes", align_bytes=64)
+        nc.vector.tensor_copy(x_codes[:], word_table[:].bitcast(U32).indirect(offsets[:]))
+
+        w_codes = shared.tile([P, N], U32, name="w_codes", align_bytes=64, offset=S)
+        w_scale = sb.tile([P, N], U8, name="w_scale", align_bytes=64)
+        nc.vector.quantize_mx(
+            out=w_codes[:].bitcast(FP8X4), scales=w_scale[:], in_=w_grouped[:].rearrange("p n j -> p (n j)")
+        )
+
+        scaled = []
+        x_scale = shared.tile([P, S], U8, name="x_scale", align_bytes=64, offset=0)
+        for n, (lo, hi) in enumerate(PIECES):
+            nc.vector.tensor_copy(x_scale[:, lo:hi], scale_table[:].indirect(offsets[:, lo // 16 : hi // 16]))
+            acc = ps.tile([P, hi - lo], F32, name=f"acc{n}", tag=ACC_TAG[n])
+            nc.tensor.matmul_mx(
+                out=acc[:],
+                lhsT=w_codes[:].bitcast(FP8X4),
+                lhsT_scale=w_scale[:],
+                rhs=x_codes[:, lo:hi].bitcast(FP8X4),
+                rhs_scale=x_scale[:, lo:hi],
+                start=True,
+                stop=True,
+            )
+            scaled.append(acc)
+
+        for n, (lo, hi) in enumerate(PIECES):
+            h, at = divmod(lo, HALF)
+            z = sb.tile([P, hi - lo], F32, name=f"scaled{n}", align_bytes=64)
+            nc.vector.tensor_tensor(z[:], scaled[n][:], inv_rows[h][:, at : at + hi - lo], MULT)
+            scaled[n] = z
+        for n, (lo, hi) in enumerate(PIECES):
+            h, at = divmod(lo, HALF)
+            result = sb.tile([P, hi - lo], F32, name=f"result{n}", align_bytes=64)
+            nc.vector.tensor_tensor(result[:], scaled[n][:], shift_rows[h][:, at : at + hi - lo], ADD)
+            nc.sync.dma_start(out=out[:, lo:hi], in_=result[:])

@@ -24,7 +24,7 @@ HALF = S // 2
 BLOCKS = HALF // P
 MEAN_ROW, INV_ROW = P - 2, P - 1
 PIECES = [(0, 256), (256, 384), (384, 512)]
-ACC_TAG = ["acc0", "acc1", "turned0"]
+ACC_TAG = ["inv_ps0", "prod_ps0", "inv_ps1"]
 
 
 def tile_picked_lnfold_none_p_kernel(
@@ -47,33 +47,29 @@ def tile_picked_lnfold_none_p_kernel(
         nc.sync.dma_start(out=stat_table[INV_ROW : INV_ROW + 1, :], in_=inv[0:1, :])
         nc.vector.memset(stat_table[0:MEAN_ROW, :], 0.0)
 
+        w_raw = sb.tile([P, PACK, N], F32, name="w_raw", align_bytes=64)
+        nc.sync.dma_start(out=w_raw[:], in_=w1.rearrange("(p j) n -> p j n", j=PACK))
         word_table = sb.tile([P, T], I32, name="word_table", align_bytes=64)
         nc.sync.dma_start(out=word_table[:], in_=x_words[0].rearrange("p n t -> p (n t)").bitcast(I32))
 
+        gsum_col = sb.tile([P, 1], F32, name="gsum_col")
+        bias_col = sb.tile([P, 1], F32, name="bias_col")
+        with nc.allow_non_contiguous_dma(reason="one value a partition"):
+            nc.sync.dma_start(out=gsum_col[:], in_=gsum)
+            nc.sync.dma_start(out=bias_col[:], in_=b)
+
         scale_table = sb.tile([P, T], U8, name="scale_table", align_bytes=64)
         nc.vector.memset(scale_table[:].bitcast(I32), 0)
-        w_raw = sb.tile([P, PACK, N], F32, name="w_raw", align_bytes=64)
-        nc.sync.dma_start(out=w_raw[:], in_=w1.rearrange("(p j) n -> p j n", j=PACK))
         for q in range(4):
             nc.sync.dma_start(
                 out=scale_table[32 * q : 32 * q + 4, :].bitcast(I32),
                 in_=x_scales[0, 4 * q : 4 * q + 4, :].bitcast(I32),
             )
         identity = sb.tile([P, P], F32, name="identity", align_bytes=64)
-        nc.vector.memset(identity[:], 0.0)
-        make_identity(nc, identity[:], nomemset=True)
-
-        gsum_col = sb.tile([P, 1], F32, name="gsum_col")
-        bias_col = sb.tile([P, 1], F32, name="bias_col")
-        with nc.allow_non_contiguous_dma(reason="one value a partition"):
-            nc.scalar.dma_start(out=gsum_col[:], in_=gsum)
-            nc.scalar.dma_start(out=bias_col[:], in_=b)
+        make_identity(nc, identity[:])
 
         w_grouped = sb.tile([P, N, PACK], BF16, name="w_grouped", align_bytes=64)
         nc.scalar.activation(w_grouped[:], w_raw[:].rearrange("p j n -> p n j"), COPY)
-
-        neg_gsum = sb.tile([P, 1], F32, name="neg_gsum")
-        nc.scalar.activation(neg_gsum[:], gsum_col[:], COPY, scale=-1.0)
 
         inv_rows, shift_rows = [], []
         for h in range(2):
@@ -82,20 +78,19 @@ def tile_picked_lnfold_none_p_kernel(
             turned = ps.tile([P, BLOCKS, P], F32, name=f"turned{h}")
             for c in range(BLOCKS):
                 nc.tensor.transpose(turned[:, c, :], picked[:, c * P : (c + 1) * P], identity[:])
-            cols = sb.tile([P, BLOCKS, 2], F32, name=f"cols{h}")
-            nc.scalar.copy(out=cols[:], in_=turned[:, :, MEAN_ROW:P])
+            neg_inv = sb.tile([P, BLOCKS], F32, name=f"neg_inv{h}")
+            nc.scalar.activation(neg_inv[:], turned[:, :, INV_ROW], COPY, scale=-1.0)
             prod = sb.tile([P, BLOCKS], F32, name=f"prod{h}")
             for c in range(BLOCKS):
                 nc.scalar.activation(
-                    prod[:, c : c + 1], cols[:, c, 0:1], COPY,
-                    scale=cols[:, c, 1:2],
+                    prod[:, c : c + 1], turned[:, c, MEAN_ROW : MEAN_ROW + 1], COPY, scale=neg_inv[:, c : c + 1]
                 )
-            inv_ps = ps.tile([P, HALF], F32, name=f"inv_ps{h}")
-            prod_ps = ps.tile([P, HALF], F32, name=f"prod_ps{h}")
+            inv_ps = ps.tile([P, HALF], F32, name=f"inv_ps{h}", tag=f"inv_ps{h}")
+            prod_ps = ps.tile([P, HALF], F32, name=f"prod_ps{h}", tag=f"prod_ps{h}")
             for c in range(BLOCKS):
                 nc.tensor.transpose(
                     inv_ps[:, c * P : (c + 1) * P],
-                    cols[:, c, 1:2].to_broadcast([P, P]),
+                    neg_inv[:, c : c + 1].to_broadcast([P, P]),
                     identity[:],
                 )
             for c in range(BLOCKS):
@@ -103,20 +98,20 @@ def tile_picked_lnfold_none_p_kernel(
                     prod_ps[:, c * P : (c + 1) * P], prod[:, c : c + 1].to_broadcast([P, P]), identity[:]
                 )
             inv_row = sb.tile([P, HALF], F32, name=f"inv_row{h}", align_bytes=64)
-            nc.scalar.copy(out=inv_row[:], in_=inv_ps[:])
+            nc.scalar.activation(inv_row[:], inv_ps[:], COPY, scale=-1.0)
             shift_row = sb.tile([P, HALF], F32, name=f"shift_row{h}", align_bytes=64)
-            nc.scalar.activation(shift_row[:], prod_ps[:], IDENTITY, bias=bias_col[:], scale=neg_gsum[:])
+            nc.scalar.activation(shift_row[:], prod_ps[:], IDENTITY, bias=bias_col[:], scale=gsum_col[:])
             inv_rows.append(inv_row)
             shift_rows.append(shift_row)
-
-        x_codes = sb.tile([P, S], U32, name="x_codes", align_bytes=64)
-        nc.vector.tensor_copy(x_codes[:], word_table[:].bitcast(U32).indirect(offsets[:]))
 
         w_codes = shared.tile([P, N], U32, name="w_codes", align_bytes=64, offset=S)
         w_scale = sb.tile([P, N], U8, name="w_scale", align_bytes=64)
         nc.vector.quantize_mx(
             out=w_codes[:].bitcast(FP8X4), scales=w_scale[:], in_=w_grouped[:].rearrange("p n j -> p (n j)")
         )
+
+        x_codes = shared.tile([P, S], U32, name="x_codes", align_bytes=64, offset=4 * T)
+        nc.vector.tensor_copy(x_codes[:], word_table[:].bitcast(U32).indirect(offsets[:]))
 
         scaled = []
         x_scale = shared.tile([P, S], U8, name="x_scale", align_bytes=64, offset=0)
@@ -134,13 +129,26 @@ def tile_picked_lnfold_none_p_kernel(
             )
             scaled.append(acc)
 
-        for n, (lo, hi) in enumerate(PIECES):
+        def scale_piece(n):
+            lo, hi = PIECES[n]
             h, at = divmod(lo, HALF)
             z = sb.tile([P, hi - lo], F32, name=f"scaled{n}", align_bytes=64)
             nc.vector.tensor_tensor(z[:], scaled[n][:], inv_rows[h][:, at : at + hi - lo], MULT)
             scaled[n] = z
-        for n, (lo, hi) in enumerate(PIECES):
+
+        def finish_piece(n):
+            lo, hi = PIECES[n]
             h, at = divmod(lo, HALF)
-            result = sb.tile([P, hi - lo], F32, name=f"result{n}", align_bytes=64)
+            if n == 1:
+                result = shared.tile([P, hi - lo], F32, name=f"result{n}", align_bytes=64, offset=4 * T)
+            else:
+                result = sb.tile([P, hi - lo], F32, name=f"result{n}", align_bytes=64)
             nc.vector.tensor_tensor(result[:], scaled[n][:], shift_rows[h][:, at : at + hi - lo], ADD)
             nc.sync.dma_start(out=out[:, lo:hi], in_=result[:])
+
+        scale_piece(0)
+        scale_piece(1)
+        finish_piece(0)
+        scale_piece(2)
+        finish_piece(1)
+        finish_piece(2)

@@ -20,11 +20,18 @@ IDENTITY = mybir.ActivationFunctionType.Identity
 
 P = 128
 PACK = 4
+QUADRANT = 32
+GROUP = 16
 HALF = S // 2
 BLOCKS = HALF // P
+
 MEAN_ROW, INV_ROW = P - 2, P - 1
+
 PIECES = [(0, 256), (256, 384), (384, 512)]
-ACC_TAG = ["inv_ps0", "prod_ps0", "inv_ps1"]
+SUM_BANKS = ["turned1", "inv_ps0", "prod_ps0"]
+
+STAT_AT, X_SCALE_AT, W_CODES_AT, X_CODES_AT = 0, 0, S, 4 * T
+LATE_PIECE = 1
 
 
 def tile_picked_lnfold_none_p_kernel(
@@ -36,21 +43,22 @@ def tile_picked_lnfold_none_p_kernel(
         shared = ctx.enter_context(tc.tile_pool(name="shared", bufs=1))
         ps = ctx.enter_context(tc.psum_pool(name="ps", bufs=1))
 
-        offsets = sb.tile([P, S // 16], U16, name="offsets")
+        offsets = sb.tile([P, S // GROUP], U16, name="offsets")
         nc.sync.dma_start(offsets[:], offs)
 
-        def entries(h):
-            return offsets[:, h * HALF // 16 : (h + 1) * HALF // 16]
+        def entries(lo, hi):
+            return offsets[:, lo // GROUP : hi // GROUP]
 
-        stat_table = shared.tile([P, T], F32, name="stat_table", align_bytes=64, offset=0)
+        stat_table = shared.tile([P, T], F32, name="stat_table", align_bytes=64, offset=STAT_AT)
         nc.sync.dma_start(out=stat_table[MEAN_ROW : MEAN_ROW + 1, :], in_=mean[0:1, :])
         nc.sync.dma_start(out=stat_table[INV_ROW : INV_ROW + 1, :], in_=inv[0:1, :])
         nc.vector.memset(stat_table[0:MEAN_ROW, :], 0.0)
 
-        w_raw = sb.tile([P, PACK, N], F32, name="w_raw", align_bytes=64)
-        nc.sync.dma_start(out=w_raw[:], in_=w1.rearrange("(p j) n -> p j n", j=PACK))
         word_table = sb.tile([P, T], I32, name="word_table", align_bytes=64)
         nc.sync.dma_start(out=word_table[:], in_=x_words[0].rearrange("p n t -> p (n t)").bitcast(I32))
+
+        w_raw = sb.tile([P, PACK, N], F32, name="w_raw", align_bytes=64)
+        nc.sync.dma_start(out=w_raw[:], in_=w1.rearrange("(p j) n -> p j n", j=PACK))
 
         gsum_col = sb.tile([P, 1], F32, name="gsum_col")
         bias_col = sb.tile([P, 1], F32, name="bias_col")
@@ -60,43 +68,42 @@ def tile_picked_lnfold_none_p_kernel(
 
         scale_table = sb.tile([P, T], U8, name="scale_table", align_bytes=64)
         nc.vector.memset(scale_table[:].bitcast(I32), 0)
-        for q in range(4):
+        for q in range(P // QUADRANT):
             nc.sync.dma_start(
-                out=scale_table[32 * q : 32 * q + 4, :].bitcast(I32),
-                in_=x_scales[0, 4 * q : 4 * q + 4, :].bitcast(I32),
+                out=scale_table[QUADRANT * q : QUADRANT * q + PACK, :].bitcast(I32),
+                in_=x_scales[0, PACK * q : PACK * (q + 1), :].bitcast(I32),
             )
         identity = sb.tile([P, P], F32, name="identity", align_bytes=64)
         make_identity(nc, identity[:])
 
         w_grouped = sb.tile([P, N, PACK], BF16, name="w_grouped", align_bytes=64)
-        nc.scalar.activation(w_grouped[:], w_raw[:].rearrange("p j n -> p n j"), COPY)
+        nc.gpsimd.tensor_copy(w_grouped[:], w_raw[:].rearrange("p j n -> p n j"))
 
         inv_rows, shift_rows = [], []
-        for h in range(2):
+        for h in range(S // HALF):
             picked = sb.tile([P, HALF], F32, name=f"picked{h}", align_bytes=64)
-            nc.vector.tensor_copy(picked[:], stat_table[:].indirect(entries(h)))
-            turned = ps.tile([P, BLOCKS, P], F32, name=f"turned{h}")
+            nc.vector.tensor_copy(picked[:], stat_table[:].indirect(entries(h * HALF, (h + 1) * HALF)))
+
+            turned = ps.tile([P, BLOCKS, P], F32, name=f"turned{h}", tag=f"turned{h}")
             for c in range(BLOCKS):
                 nc.tensor.transpose(turned[:, c, :], picked[:, c * P : (c + 1) * P], identity[:])
+
             neg_inv = sb.tile([P, BLOCKS], F32, name=f"neg_inv{h}")
             nc.scalar.activation(neg_inv[:], turned[:, :, INV_ROW], COPY, scale=-1.0)
-            prod = sb.tile([P, BLOCKS], F32, name=f"prod{h}")
+            neg_prod = sb.tile([P, BLOCKS], F32, name=f"prod{h}")
             for c in range(BLOCKS):
                 nc.scalar.activation(
-                    prod[:, c : c + 1], turned[:, c, MEAN_ROW : MEAN_ROW + 1], COPY, scale=neg_inv[:, c : c + 1]
+                    neg_prod[:, c : c + 1], turned[:, c, MEAN_ROW : MEAN_ROW + 1], COPY, scale=neg_inv[:, c : c + 1]
                 )
+
             inv_ps = ps.tile([P, HALF], F32, name=f"inv_ps{h}", tag=f"inv_ps{h}")
             prod_ps = ps.tile([P, HALF], F32, name=f"prod_ps{h}", tag=f"prod_ps{h}")
-            for c in range(BLOCKS):
-                nc.tensor.transpose(
-                    inv_ps[:, c * P : (c + 1) * P],
-                    neg_inv[:, c : c + 1].to_broadcast([P, P]),
-                    identity[:],
-                )
-            for c in range(BLOCKS):
-                nc.tensor.transpose(
-                    prod_ps[:, c * P : (c + 1) * P], prod[:, c : c + 1].to_broadcast([P, P]), identity[:]
-                )
+            for spread, column in ((inv_ps, neg_inv), (prod_ps, neg_prod)):
+                for c in range(BLOCKS):
+                    nc.tensor.transpose(
+                        spread[:, c * P : (c + 1) * P], column[:, c : c + 1].to_broadcast([P, P]), identity[:]
+                    )
+
             inv_row = sb.tile([P, HALF], F32, name=f"inv_row{h}", align_bytes=64)
             nc.scalar.activation(inv_row[:], inv_ps[:], COPY, scale=-1.0)
             shift_row = sb.tile([P, HALF], F32, name=f"shift_row{h}", align_bytes=64)
@@ -104,20 +111,20 @@ def tile_picked_lnfold_none_p_kernel(
             inv_rows.append(inv_row)
             shift_rows.append(shift_row)
 
-        w_codes = shared.tile([P, N], U32, name="w_codes", align_bytes=64, offset=S)
+        x_codes = shared.tile([P, S], U32, name="x_codes", align_bytes=64, offset=X_CODES_AT)
+        nc.vector.tensor_copy(x_codes[:], word_table[:].bitcast(U32).indirect(offsets[:]))
+
+        w_codes = shared.tile([P, N], U32, name="w_codes", align_bytes=64, offset=W_CODES_AT)
         w_scale = sb.tile([P, N], U8, name="w_scale", align_bytes=64)
         nc.vector.quantize_mx(
             out=w_codes[:].bitcast(FP8X4), scales=w_scale[:], in_=w_grouped[:].rearrange("p n j -> p (n j)")
         )
 
-        x_codes = shared.tile([P, S], U32, name="x_codes", align_bytes=64, offset=4 * T)
-        nc.vector.tensor_copy(x_codes[:], word_table[:].bitcast(U32).indirect(offsets[:]))
-
-        scaled = []
-        x_scale = shared.tile([P, S], U8, name="x_scale", align_bytes=64, offset=0)
+        x_scale = shared.tile([P, S], U8, name="x_scale", align_bytes=64, offset=X_SCALE_AT)
+        sums = []
         for n, (lo, hi) in enumerate(PIECES):
-            nc.vector.tensor_copy(x_scale[:, lo:hi], scale_table[:].indirect(offsets[:, lo // 16 : hi // 16]))
-            acc = ps.tile([P, hi - lo], F32, name=f"acc{n}", tag=ACC_TAG[n])
+            nc.vector.tensor_copy(x_scale[:, lo:hi], scale_table[:].indirect(entries(lo, hi)))
+            acc = ps.tile([P, hi - lo], F32, name=f"acc{n}", tag=SUM_BANKS[n])
             nc.tensor.matmul_mx(
                 out=acc[:],
                 lhsT=w_codes[:].bitcast(FP8X4),
@@ -127,28 +134,31 @@ def tile_picked_lnfold_none_p_kernel(
                 start=True,
                 stop=True,
             )
-            scaled.append(acc)
+            sums.append(acc)
+
+        def part(rows, n):
+            lo, hi = PIECES[n]
+            h, at = divmod(lo, HALF)
+            return rows[h][:, at : at + hi - lo]
 
         def scale_piece(n):
             lo, hi = PIECES[n]
-            h, at = divmod(lo, HALF)
-            z = sb.tile([P, hi - lo], F32, name=f"scaled{n}", align_bytes=64)
-            nc.vector.tensor_tensor(z[:], scaled[n][:], inv_rows[h][:, at : at + hi - lo], MULT)
-            scaled[n] = z
+            scaled = sb.tile([P, hi - lo], F32, name=f"scaled{n}", align_bytes=64)
+            nc.vector.tensor_tensor(scaled[:], sums[n][:], part(inv_rows, n), MULT)
+            return scaled
 
-        def finish_piece(n):
+        def shift_and_store(n, scaled):
             lo, hi = PIECES[n]
-            h, at = divmod(lo, HALF)
-            if n == 1:
-                result = shared.tile([P, hi - lo], F32, name=f"result{n}", align_bytes=64, offset=4 * T)
+            if n == LATE_PIECE:
+                result = shared.tile([P, hi - lo], F32, name=f"result{n}", align_bytes=64, offset=X_CODES_AT)
             else:
                 result = sb.tile([P, hi - lo], F32, name=f"result{n}", align_bytes=64)
-            nc.vector.tensor_tensor(result[:], scaled[n][:], shift_rows[h][:, at : at + hi - lo], ADD)
+            nc.vector.tensor_tensor(result[:], scaled[:], part(shift_rows, n), ADD)
             nc.sync.dma_start(out=out[:, lo:hi], in_=result[:])
 
-        scale_piece(0)
-        scale_piece(1)
-        finish_piece(0)
-        scale_piece(2)
-        finish_piece(1)
-        finish_piece(2)
+        waiting = scale_piece(0)
+        for n in range(1, len(PIECES)):
+            ahead = scale_piece(n)
+            shift_and_store(n - 1, waiting)
+            waiting = ahead
+        shift_and_store(len(PIECES) - 1, waiting)

@@ -51,7 +51,7 @@ def tile_picked_lnfold_none_p_kernel(
 
         stat_table = shared.tile([P, T], F32, name="stat_table", align_bytes=64, offset=STAT_AT)
         nc.sync.dma_start(out=stat_table[MEAN_ROW : MEAN_ROW + 1, :], in_=mean[0:1, :])
-        nc.sync.dma_start(out=stat_table[INV_ROW : INV_ROW + 1, :], in_=inv[0:1, :])
+        nc.scalar.dma_start(out=stat_table[INV_ROW : INV_ROW + 1, :], in_=inv[0:1, :])
         nc.vector.memset(stat_table[0:MEAN_ROW, :], 0.0)
 
         word_table = sb.tile([P, T], I32, name="word_table", align_bytes=64)

@@ -24,14 +24,10 @@ QUADRANT = 32
 GROUP = 16
 HALF = S // 2
 BLOCKS = HALF // P
-
 MEAN_ROW, INV_ROW = P - 2, P - 1
-
+STAT_PIECES = [(0, 128), (128, 256), (256, 512)]
 PIECES = [(0, 256), (256, 384), (384, 512)]
-SUM_BANKS = ["turned1", "inv_ps0", "prod_ps0"]
-
-STAT_AT, X_SCALE_AT, W_CODES_AT, X_CODES_AT = 0, 0, S, 4 * T
-LATE_PIECE = 1
+SUM_BANKS = ["turned2", "turned1", "turned0"]
 
 
 def tile_picked_lnfold_none_p_kernel(
@@ -49,14 +45,13 @@ def tile_picked_lnfold_none_p_kernel(
         def entries(lo, hi):
             return offsets[:, lo // GROUP : hi // GROUP]
 
-        stat_table = shared.tile([P, T], F32, name="stat_table", align_bytes=64, offset=STAT_AT)
-        nc.sync.dma_start(out=stat_table[MEAN_ROW : MEAN_ROW + 1, :], in_=mean[0:1, :])
+        stat_table = shared.tile([P, T], F32, name="stat_table", align_bytes=64, offset=0)
         nc.scalar.dma_start(out=stat_table[INV_ROW : INV_ROW + 1, :], in_=inv[0:1, :])
+        nc.sync.dma_start(out=stat_table[MEAN_ROW : MEAN_ROW + 1, :], in_=mean[0:1, :])
         nc.vector.memset(stat_table[0:MEAN_ROW, :], 0.0)
 
         word_table = sb.tile([P, T], I32, name="word_table", align_bytes=64)
         nc.sync.dma_start(out=word_table[:], in_=x_words[0].rearrange("p n t -> p (n t)").bitcast(I32))
-
         w_raw = sb.tile([P, PACK, N], F32, name="w_raw", align_bytes=64)
         nc.sync.dma_start(out=w_raw[:], in_=w1.rearrange("(p j) n -> p j n", j=PACK))
 
@@ -73,64 +68,79 @@ def tile_picked_lnfold_none_p_kernel(
                 out=scale_table[QUADRANT * q : QUADRANT * q + PACK, :].bitcast(I32),
                 in_=x_scales[0, PACK * q : PACK * (q + 1), :].bitcast(I32),
             )
+
         identity = sb.tile([P, P], F32, name="identity", align_bytes=64)
         make_identity(nc, identity[:])
+        warm = sb.tile([P, 1], F32, name="warm")
+        nc.scalar.activation(warm[0:32, :], stat_table[0:32, 0:1], COPY)
 
         w_grouped = sb.tile([P, N, PACK], BF16, name="w_grouped", align_bytes=64)
         nc.gpsimd.tensor_copy(w_grouped[:], w_raw[:].rearrange("p j n -> p n j"))
 
-        inv_rows, shift_rows = [], []
-        for h in range(S // HALF):
-            picked = sb.tile([P, HALF], F32, name=f"picked{h}", align_bytes=64)
-            nc.vector.tensor_copy(picked[:], stat_table[:].indirect(entries(h * HALF, (h + 1) * HALF)))
+        picked = []
+        for s, (lo, hi) in enumerate(STAT_PIECES):
+            pick = sb.tile([P, hi - lo], F32, name=f"picked{s}", align_bytes=64)
+            looked_up = stat_table[:].indirect(entries(lo, hi))
+            if hi <= HALF:
+                nc.vector.tensor_copy(pick[:], looked_up)
+            else:
+                nc.scalar.activation(pick[:], looked_up, COPY)
+            picked.append(pick)
 
-            turned = ps.tile([P, BLOCKS, P], F32, name=f"turned{h}", tag=f"turned{h}")
-            for c in range(BLOCKS):
-                nc.tensor.transpose(turned[:, c, :], picked[:, c * P : (c + 1) * P], identity[:])
-
-            neg_inv = sb.tile([P, BLOCKS], F32, name=f"neg_inv{h}")
-            nc.scalar.activation(neg_inv[:], turned[:, :, INV_ROW], COPY, scale=-1.0)
-            neg_prod = sb.tile([P, BLOCKS], F32, name=f"prod{h}")
-            for c in range(BLOCKS):
-                nc.scalar.activation(
-                    neg_prod[:, c : c + 1], turned[:, c, MEAN_ROW : MEAN_ROW + 1], COPY, scale=neg_inv[:, c : c + 1]
-                )
-
-            inv_ps = ps.tile([P, HALF], F32, name=f"inv_ps{h}", tag=f"inv_ps{h}")
-            prod_ps = ps.tile([P, HALF], F32, name=f"prod_ps{h}", tag=f"prod_ps{h}")
-            for spread, column in ((inv_ps, neg_inv), (prod_ps, neg_prod)):
-                for c in range(BLOCKS):
-                    nc.tensor.transpose(
-                        spread[:, c * P : (c + 1) * P], column[:, c : c + 1].to_broadcast([P, P]), identity[:]
-                    )
-
-            inv_row = sb.tile([P, HALF], F32, name=f"inv_row{h}", align_bytes=64)
-            nc.scalar.activation(inv_row[:], inv_ps[:], COPY, scale=-1.0)
-            shift_row = sb.tile([P, HALF], F32, name=f"shift_row{h}", align_bytes=64)
-            nc.scalar.activation(shift_row[:], prod_ps[:], IDENTITY, bias=bias_col[:], scale=gsum_col[:])
-            inv_rows.append(inv_row)
-            shift_rows.append(shift_row)
-
-        x_codes = shared.tile([P, S], U32, name="x_codes", align_bytes=64, offset=X_CODES_AT)
+        x_codes = shared.tile([P, S], U32, name="x_codes", align_bytes=64, offset=4 * T)
         nc.vector.tensor_copy(x_codes[:], word_table[:].bitcast(U32).indirect(offsets[:]))
 
-        w_codes = shared.tile([P, N], U32, name="w_codes", align_bytes=64, offset=W_CODES_AT)
+        means, neg_inv, neg_prod = [], [], []
+        for s, (lo, hi) in enumerate(STAT_PIECES):
+            blocks = (hi - lo) // P
+            turn = ps.tile([P, blocks, P], F32, name=f"turned{s}", tag=f"turned{s}")
+            for c in range(blocks):
+                nc.tensor.transpose(turn[:, c, :], picked[s][:, c * P : (c + 1) * P], identity[:])
+            column = sb.tile([P, blocks], F32, name=f"neg_inv{s}")
+            nc.scalar.activation(column[:], turn[:, :, INV_ROW], COPY, scale=-1.0)
+            for c in range(blocks):
+                means.append(turn[:, c, MEAN_ROW : MEAN_ROW + 1])
+                neg_inv.append(column[:, c : c + 1])
+        for c in range(S // P):
+            prod = sb.tile([P, 1], F32, name=f"neg_prod{c}")
+            nc.scalar.activation(prod[:], means[c], COPY, scale=neg_inv[c])
+            neg_prod.append(prod[:])
+
+        def spread(name, columns):
+            rows_ps = ps.tile([P, HALF], F32, name=name, tag=name)
+            for c, column in enumerate(columns):
+                nc.tensor.transpose(rows_ps[:, c * P : (c + 1) * P], column.to_broadcast([P, P]), identity[:])
+            return rows_ps
+
+        inv_rows, shift_rows = [], []
+        for h in range(S // HALF):
+            inv_ps = spread(f"inv_ps{h}", neg_inv[h * BLOCKS : (h + 1) * BLOCKS])
+            inv_row = sb.tile([P, HALF], F32, name=f"inv_row{h}", align_bytes=64)
+            nc.scalar.activation(inv_row[:], inv_ps[:], COPY, scale=-1.0)
+            inv_rows.append(inv_row)
+        for h in range(S // HALF):
+            prod_ps = spread(f"prod_ps{h}", neg_prod[h * BLOCKS : (h + 1) * BLOCKS])
+            shift_row = sb.tile([P, HALF], F32, name=f"shift_row{h}", align_bytes=64)
+            nc.scalar.activation(shift_row[:], prod_ps[:], IDENTITY, bias=bias_col[:], scale=gsum_col[:])
+            shift_rows.append(shift_row)
+
+        w_codes = shared.tile([P, N], U32, name="w_codes", align_bytes=64, offset=S)
         w_scale = sb.tile([P, N], U8, name="w_scale", align_bytes=64)
         nc.vector.quantize_mx(
             out=w_codes[:].bitcast(FP8X4), scales=w_scale[:], in_=w_grouped[:].rearrange("p n j -> p (n j)")
         )
 
-        x_scale = shared.tile([P, S], U8, name="x_scale", align_bytes=64, offset=X_SCALE_AT)
         sums = []
         for n, (lo, hi) in enumerate(PIECES):
-            nc.vector.tensor_copy(x_scale[:, lo:hi], scale_table[:].indirect(entries(lo, hi)))
+            x_scale = shared.tile([P, hi - lo], U8, name=f"x_scale{n}", align_bytes=64, offset=lo)
+            nc.vector.tensor_copy(x_scale[:], scale_table[:].indirect(entries(lo, hi)))
             acc = ps.tile([P, hi - lo], F32, name=f"acc{n}", tag=SUM_BANKS[n])
             nc.tensor.matmul_mx(
                 out=acc[:],
                 lhsT=w_codes[:].bitcast(FP8X4),
                 lhsT_scale=w_scale[:],
                 rhs=x_codes[:, lo:hi].bitcast(FP8X4),
-                rhs_scale=x_scale[:, lo:hi],
+                rhs_scale=x_scale[:],
                 start=True,
                 stop=True,
             )
@@ -149,8 +159,8 @@ def tile_picked_lnfold_none_p_kernel(
 
         def shift_and_store(n, scaled):
             lo, hi = PIECES[n]
-            if n == LATE_PIECE:
-                result = shared.tile([P, hi - lo], F32, name=f"result{n}", align_bytes=64, offset=X_CODES_AT)
+            if n == 1:
+                result = shared.tile([P, hi - lo], F32, name=f"result{n}", align_bytes=64, offset=4 * T)
             else:
                 result = sb.tile([P, hi - lo], F32, name=f"result{n}", align_bytes=64)
             nc.vector.tensor_tensor(result[:], scaled[:], part(shift_rows, n), ADD)

@@ -48,26 +48,26 @@ def tile_picked_lnfold_none_p_kernel(
         stat_table = shared.tile([P, T], F32, name="stat_table", align_bytes=64, offset=0)
         nc.scalar.dma_start(out=stat_table[INV_ROW : INV_ROW + 1, :], in_=inv[0:1, :])
         nc.sync.dma_start(out=stat_table[MEAN_ROW : MEAN_ROW + 1, :], in_=mean[0:1, :])
+        scale_table = sb.tile([P, T], U8, name="scale_table", align_bytes=64)
+        nc.vector.memset(scale_table[:].bitcast(I32), 0)
         nc.vector.memset(stat_table[0:MEAN_ROW, :], 0.0)
 
         word_table = sb.tile([P, T], I32, name="word_table", align_bytes=64)
         nc.sync.dma_start(out=word_table[:], in_=x_words[0].rearrange("p n t -> p (n t)").bitcast(I32))
-        w_raw = sb.tile([P, PACK, N], F32, name="w_raw", align_bytes=64)
+        w_raw = shared.tile([P, PACK, N], F32, name="w_raw", align_bytes=64, offset=6 * T)
         nc.sync.dma_start(out=w_raw[:], in_=w1.rearrange("(p j) n -> p j n", j=PACK))
+
+        for q in range(P // QUADRANT):
+            nc.sync.dma_start(
+                out=scale_table[QUADRANT * q : QUADRANT * q + PACK, :].bitcast(I32),
+                in_=x_scales[0, PACK * q : PACK * (q + 1), :].bitcast(I32),
+            )
 
         gsum_col = sb.tile([P, 1], F32, name="gsum_col")
         bias_col = sb.tile([P, 1], F32, name="bias_col")
         with nc.allow_non_contiguous_dma(reason="one value a partition"):
             nc.sync.dma_start(out=gsum_col[:], in_=gsum)
             nc.sync.dma_start(out=bias_col[:], in_=b)
-
-        scale_table = sb.tile([P, T], U8, name="scale_table", align_bytes=64)
-        nc.vector.memset(scale_table[:].bitcast(I32), 0)
-        for q in range(P // QUADRANT):
-            nc.sync.dma_start(
-                out=scale_table[QUADRANT * q : QUADRANT * q + PACK, :].bitcast(I32),
-                in_=x_scales[0, PACK * q : PACK * (q + 1), :].bitcast(I32),
-            )
 
         identity = sb.tile([P, P], F32, name="identity", align_bytes=64)
         make_identity(nc, identity[:])
@@ -126,14 +126,15 @@ def tile_picked_lnfold_none_p_kernel(
 
         w_codes = shared.tile([P, N], U32, name="w_codes", align_bytes=64, offset=S)
         w_scale = sb.tile([P, N], U8, name="w_scale", align_bytes=64)
-        nc.vector.quantize_mx(
-            out=w_codes[:].bitcast(FP8X4), scales=w_scale[:], in_=w_grouped[:].rearrange("p n j -> p (n j)")
-        )
 
         sums = []
         for n, (lo, hi) in enumerate(PIECES):
-            x_scale = shared.tile([P, hi - lo], U8, name=f"x_scale{n}", align_bytes=64, offset=lo)
+            x_scale = shared.tile([P, hi - lo], U8, name=f"x_scale{n}", align_bytes=64, offset=(6 * T if n else 0) + lo)
             nc.vector.tensor_copy(x_scale[:], scale_table[:].indirect(entries(lo, hi)))
+            if n == 0:
+                nc.vector.quantize_mx(
+                    out=w_codes[:].bitcast(FP8X4), scales=w_scale[:], in_=w_grouped[:].rearrange("p n j -> p (n j)")
+                )
             acc = ps.tile([P, hi - lo], F32, name=f"acc{n}", tag=SUM_BANKS[n])
             nc.tensor.matmul_mx(
                 out=acc[:],

@@ -22,12 +22,12 @@ P = 128
 PACK = 4
 QUADRANT = 32
 GROUP = 16
-HALF = S // 2
-BLOCKS = HALF // P
+BLOCKS = S // P
 MEAN_ROW, INV_ROW = P - 2, P - 1
-STAT_PIECES = [(0, 128), (128, 256), (256, 512)]
-PIECES = [(0, 256), (256, 384), (384, 512)]
-SUM_BANKS = ["turned2", "turned1", "turned0"]
+STAT_PIECES = [(0, 128), (128, 256), (256, 384), (384, 512)]
+ORDER = [3, 0, 1, 2]
+SPREAD = S - P
+SUM_BANKS = ["turned3", "turned0", "turned1", "acc3"]
 
 
 def tile_picked_lnfold_none_p_kernel(
@@ -81,7 +81,7 @@ def tile_picked_lnfold_none_p_kernel(
         for s, (lo, hi) in enumerate(STAT_PIECES):
             pick = sb.tile([P, hi - lo], F32, name=f"picked{s}", align_bytes=64)
             looked_up = stat_table[:].indirect(entries(lo, hi))
-            if hi <= HALF:
+            if s < 2:
                 nc.vector.tensor_copy(pick[:], looked_up)
             else:
                 nc.scalar.activation(pick[:], looked_up, COPY)
@@ -96,80 +96,91 @@ def tile_picked_lnfold_none_p_kernel(
             turn = ps.tile([P, blocks, P], F32, name=f"turned{s}", tag=f"turned{s}")
             for c in range(blocks):
                 nc.tensor.transpose(turn[:, c, :], picked[s][:, c * P : (c + 1) * P], identity[:])
+            if s == BLOCKS - 1:
+                first = sb.tile([P, 2], F32, name="first")
+                nc.scalar.activation(first[:], turn[:, 0, MEAN_ROW:], COPY)
+                continue
             column = sb.tile([P, blocks], F32, name=f"neg_inv{s}")
             nc.scalar.activation(column[:], turn[:, :, INV_ROW], COPY, scale=-1.0)
             for c in range(blocks):
                 means.append(turn[:, c, MEAN_ROW : MEAN_ROW + 1])
                 neg_inv.append(column[:, c : c + 1])
-        for c in range(S // P):
+        for c in range(BLOCKS - 1):
             prod = sb.tile([P, 1], F32, name=f"neg_prod{c}")
             nc.scalar.activation(prod[:], means[c], COPY, scale=neg_inv[c])
             neg_prod.append(prod[:])
 
-        def spread(name, columns):
-            rows_ps = ps.tile([P, HALF], F32, name=name, tag=name)
+        def spread(name, columns, bank=None):
+            rows_ps = ps.tile([P, len(columns) * P], F32, name=name, tag=bank or name)
             for c, column in enumerate(columns):
                 nc.tensor.transpose(rows_ps[:, c * P : (c + 1) * P], column.to_broadcast([P, P]), identity[:])
             return rows_ps
 
-        inv_rows, shift_rows = [], []
-        for h in range(S // HALF):
-            inv_ps = spread(f"inv_ps{h}", neg_inv[h * BLOCKS : (h + 1) * BLOCKS])
-            inv_row = sb.tile([P, HALF], F32, name=f"inv_row{h}", align_bytes=64)
-            nc.scalar.activation(inv_row[:], inv_ps[:], COPY, scale=-1.0)
-            inv_rows.append(inv_row)
-        for h in range(S // HALF):
-            prod_ps = spread(f"prod_ps{h}", neg_prod[h * BLOCKS : (h + 1) * BLOCKS])
-            shift_row = sb.tile([P, HALF], F32, name=f"shift_row{h}", align_bytes=64)
-            nc.scalar.activation(shift_row[:], prod_ps[:], IDENTITY, bias=bias_col[:], scale=gsum_col[:])
-            shift_rows.append(shift_row)
+        inv_ps = spread("inv_ps", neg_inv)
+        inv_rows = sb.tile([P, SPREAD], F32, name="inv_rows", align_bytes=64)
+        nc.scalar.activation(inv_rows[:], inv_ps[:], COPY, scale=-1.0)
+        gsum_ps = spread("gsum_ps", [gsum_col[:]], "turned2")
+        neg_gsum_rows = sb.tile([P, N], F32, name="neg_gsum_rows", align_bytes=64)
+        nc.scalar.activation(neg_gsum_rows[:], gsum_ps[:], COPY, scale=-1.0)
+        prod_ps = spread("prod_ps", neg_prod)
+        shift_rows = sb.tile([P, SPREAD], F32, name="shift_rows", align_bytes=64)
+        nc.scalar.activation(shift_rows[:], prod_ps[:], IDENTITY, bias=bias_col[:], scale=gsum_col[:])
+        term = sb.tile([P, N], F32, name="term", align_bytes=64)
+        nc.gpsimd.tensor_scalar(term[:], neg_gsum_rows[:], first[:, 0:1], first[:, 1:2], MULT, MULT)
 
         w_codes = shared.tile([P, N], U32, name="w_codes", align_bytes=64, offset=S)
         w_scale = sb.tile([P, N], U8, name="w_scale", align_bytes=64)
 
         sums = []
-        for n, (lo, hi) in enumerate(PIECES):
-            x_scale = shared.tile([P, hi - lo], U8, name=f"x_scale{n}", align_bytes=64, offset=(6 * T if n else 0) + lo)
+        for n in range(BLOCKS):
+            lo, hi = ORDER[n] * P, (ORDER[n] + 1) * P
+            x_scale = shared.tile([P, P], U8, name=f"x_scale{n}", align_bytes=64, offset=(6 * T if n else 0) + lo)
             nc.vector.tensor_copy(x_scale[:], scale_table[:].indirect(entries(lo, hi)))
             if n == 0:
                 nc.vector.quantize_mx(
                     out=w_codes[:].bitcast(FP8X4), scales=w_scale[:], in_=w_grouped[:].rearrange("p n j -> p (n j)")
                 )
-            acc = ps.tile([P, hi - lo], F32, name=f"acc{n}", tag=SUM_BANKS[n])
+            acc = ps.tile([P, P], F32, name=f"acc{n}", tag=SUM_BANKS[n])
+            tokens = (x_codes[:, lo:hi].bitcast(FP8X4), x_scale[:])
+            weights = (w_codes[:].bitcast(FP8X4), w_scale[:])
+            still, moving = (weights, tokens) if n else (tokens, weights)
             nc.tensor.matmul_mx(
                 out=acc[:],
-                lhsT=w_codes[:].bitcast(FP8X4),
-                lhsT_scale=w_scale[:],
-                rhs=x_codes[:, lo:hi].bitcast(FP8X4),
-                rhs_scale=x_scale[:],
+                lhsT=still[0],
+                lhsT_scale=still[1],
+                rhs=moving[0],
+                rhs_scale=moving[1],
                 start=True,
                 stop=True,
             )
             sums.append(acc)
+            if n == 0:
+                scaled_first = sb.tile([P, N], F32, name="scaled_first", align_bytes=64)
+                nc.scalar.activation(scaled_first[:], acc[:], COPY, scale=first[:, 1:2])
 
-        def part(rows, n):
-            lo, hi = PIECES[n]
-            h, at = divmod(lo, HALF)
-            return rows[h][:, at : at + hi - lo]
+        back = ps.tile([P, P], F32, name="back", tag="back")
+        nc.tensor.matmul(back[:], term[:], identity[:], start=True, stop=False, is_transpose=True)
+        nc.tensor.matmul(back[:], scaled_first[:], identity[:], start=False, stop=True, is_transpose=True)
+        result_first = sb.tile([P, P], F32, name="result_first", align_bytes=64)
+        nc.scalar.activation(result_first[:], back[:], IDENTITY, bias=bias_col[:])
+        nc.scalar.dma_start(out=out[:, SPREAD:S], in_=result_first[:])
 
         def scale_piece(n):
-            lo, hi = PIECES[n]
-            scaled = sb.tile([P, hi - lo], F32, name=f"scaled{n}", align_bytes=64)
-            nc.vector.tensor_tensor(scaled[:], sums[n][:], part(inv_rows, n), MULT)
+            scaled = sb.tile([P, P], F32, name=f"scaled{n}", align_bytes=64)
+            nc.vector.tensor_tensor(scaled[:], sums[n][:], inv_rows[:, (n - 1) * P : n * P], MULT)
             return scaled
 
         def shift_and_store(n, scaled):
-            lo, hi = PIECES[n]
-            if n == 1:
-                result = shared.tile([P, hi - lo], F32, name=f"result{n}", align_bytes=64, offset=4 * T)
+            if n == 2:
+                result = shared.tile([P, P], F32, name=f"result{n}", align_bytes=64, offset=4 * T)
             else:
-                result = sb.tile([P, hi - lo], F32, name=f"result{n}", align_bytes=64)
-            nc.vector.tensor_tensor(result[:], scaled[:], part(shift_rows, n), ADD)
-            nc.sync.dma_start(out=out[:, lo:hi], in_=result[:])
+                result = sb.tile([P, P], F32, name=f"result{n}", align_bytes=64)
+            nc.vector.tensor_tensor(result[:], scaled[:], shift_rows[:, (n - 1) * P : n * P], ADD)
+            nc.sync.dma_start(out=out[:, (n - 1) * P : n * P], in_=result[:])
 
-        waiting = scale_piece(0)
-        for n in range(1, len(PIECES)):
+        waiting = scale_piece(1)
+        for n in range(2, BLOCKS):
             ahead = scale_piece(n)
             shift_and_store(n - 1, waiting)
             waiting = ahead
-        shift_and_store(len(PIECES) - 1, waiting)
+        shift_and_store(BLOCKS - 1, waiting)

@@ -25,7 +25,7 @@ GROUP = 16
 BLOCKS = S // P
 MEAN_ROW, INV_ROW = P - 2, P - 1
 STAT_PIECES = [(0, 128), (128, 256), (256, 384), (384, 512)]
-ORDER = [3, 0, 1, 2]
+ORDER = [3, 0, 2, 1]
 SPREAD = S - P
 SUM_BANKS = ["turned3", "turned0", "turned1", "acc3"]
 
@@ -99,6 +99,7 @@ def tile_picked_lnfold_none_p_kernel(
             if s == BLOCKS - 1:
                 first = sb.tile([P, 2], F32, name="first")
                 nc.scalar.activation(first[:], turn[:, 0, MEAN_ROW:], COPY)
+                last_mean = turn[:, 0, MEAN_ROW : MEAN_ROW + 1]
                 continue
             column = sb.tile([P, blocks], F32, name=f"neg_inv{s}")
             nc.scalar.activation(column[:], turn[:, :, INV_ROW], COPY, scale=-1.0)
@@ -109,6 +110,9 @@ def tile_picked_lnfold_none_p_kernel(
             prod = sb.tile([P, 1], F32, name=f"neg_prod{c}")
             nc.scalar.activation(prod[:], means[c], COPY, scale=neg_inv[c])
             neg_prod.append(prod[:])
+
+        first_prod = sb.tile([P, 1], F32, name="first_prod")
+        nc.scalar.activation(first_prod[:], last_mean, COPY, scale=first[:, 1:2])
 
         def spread(name, columns, bank=None):
             rows_ps = ps.tile([P, len(columns) * P], F32, name=name, tag=bank or name)
@@ -126,7 +130,7 @@ def tile_picked_lnfold_none_p_kernel(
         shift_rows = sb.tile([P, SPREAD], F32, name="shift_rows", align_bytes=64)
         nc.scalar.activation(shift_rows[:], prod_ps[:], IDENTITY, bias=bias_col[:], scale=gsum_col[:])
         term = sb.tile([P, N], F32, name="term", align_bytes=64)
-        nc.gpsimd.tensor_scalar(term[:], neg_gsum_rows[:], first[:, 0:1], first[:, 1:2], MULT, MULT)
+        nc.scalar.activation(term[:], neg_gsum_rows[:], COPY, scale=first_prod[:])
 
         w_codes = shared.tile([P, N], U32, name="w_codes", align_bytes=64, offset=S)
         w_scale = sb.tile([P, N], U8, name="w_scale", align_bytes=64)
@@ -161,22 +165,19 @@ def tile_picked_lnfold_none_p_kernel(
         back = ps.tile([P, P], F32, name="back", tag="back")
         nc.tensor.matmul(back[:], term[:], identity[:], start=True, stop=False, is_transpose=True)
         nc.tensor.matmul(back[:], scaled_first[:], identity[:], start=False, stop=True, is_transpose=True)
-        result_first = sb.tile([P, P], F32, name="result_first", align_bytes=64)
-        nc.scalar.activation(result_first[:], back[:], IDENTITY, bias=bias_col[:])
-        nc.scalar.dma_start(out=out[:, SPREAD:S], in_=result_first[:])
+        result_pair = sb.tile([P, 2 * P], F32, name="result_pair", align_bytes=64)
+        nc.scalar.activation(result_pair[:, P:], back[:], IDENTITY, bias=bias_col[:])
 
         def scale_piece(n):
             scaled = sb.tile([P, P], F32, name=f"scaled{n}", align_bytes=64)
-            nc.vector.tensor_tensor(scaled[:], sums[n][:], inv_rows[:, (n - 1) * P : n * P], MULT)
+            nc.vector.tensor_tensor(scaled[:], sums[n][:], inv_rows[:, ORDER[n] * P : (ORDER[n] + 1) * P], MULT)
             return scaled
 
         def shift_and_store(n, scaled):
-            if n == 2:
-                result = shared.tile([P, P], F32, name=f"result{n}", align_bytes=64, offset=4 * T)
-            else:
-                result = sb.tile([P, P], F32, name=f"result{n}", align_bytes=64)
-            nc.vector.tensor_tensor(result[:], scaled[:], shift_rows[:, (n - 1) * P : n * P], ADD)
-            nc.sync.dma_start(out=out[:, (n - 1) * P : n * P], in_=result[:])
+            lo = ORDER[n] * P
+            result = result_pair if n == 2 else sb.tile([P, P], F32, name=f"result{n}", align_bytes=64)
+            nc.vector.tensor_tensor(result[:, 0:P], scaled[:], shift_rows[:, lo : lo + P], ADD)
+            nc.sync.dma_start(out=out[:, lo : lo + result.shape[1]], in_=result[:])
 
         waiting = scale_piece(1)
         for n in range(2, BLOCKS):

@@ -24,10 +24,9 @@ QUADRANT = 32
 GROUP = 16
 BLOCKS = S // P
 MEAN_ROW, INV_ROW = P - 2, P - 1
-STAT_PIECES = [(0, 128), (128, 256), (256, 384), (384, 512)]
-ORDER = [3, 0, 2, 1]
-SPREAD = S - P
-SUM_BANKS = ["turned3", "turned0", "turned1", "acc3"]
+TURNED = 2
+SPREAD = [3, 1, 0]
+CLEARED = 8
 
 
 def tile_picked_lnfold_none_p_kernel(
@@ -42,8 +41,8 @@ def tile_picked_lnfold_none_p_kernel(
         offsets = sb.tile([P, S // GROUP], U16, name="offsets")
         nc.sync.dma_start(offsets[:], offs)
 
-        def entries(lo, hi):
-            return offsets[:, lo // GROUP : hi // GROUP]
+        def entries(block, count=1):
+            return offsets[:, block * P // GROUP : (block + count) * P // GROUP]
 
         stat_table = shared.tile([P, T], F32, name="stat_table", align_bytes=64, offset=0)
         nc.scalar.dma_start(out=stat_table[INV_ROW : INV_ROW + 1, :], in_=inv[0:1, :])
@@ -70,84 +69,72 @@ def tile_picked_lnfold_none_p_kernel(
             nc.sync.dma_start(out=bias_col[:], in_=b)
 
         identity = sb.tile([P, P], F32, name="identity", align_bytes=64)
-        make_identity(nc, identity[:])
-        warm = sb.tile([P, 1], F32, name="warm")
-        nc.scalar.activation(warm[0:32, :], stat_table[0:32, 0:1], COPY)
+        nc.gpsimd.memset(identity[:, CLEARED:], 0.0)
+        nc.scalar.activation(identity[:, 0:CLEARED], identity[:, CLEARED : 2 * CLEARED], COPY)
+        make_identity(nc, identity[:], nomemset=True)
 
         w_grouped = sb.tile([P, N, PACK], BF16, name="w_grouped", align_bytes=64)
         nc.gpsimd.tensor_copy(w_grouped[:], w_raw[:].rearrange("p j n -> p n j"))
 
         picked = []
-        for s, (lo, hi) in enumerate(STAT_PIECES):
-            pick = sb.tile([P, hi - lo], F32, name=f"picked{s}", align_bytes=64)
-            looked_up = stat_table[:].indirect(entries(lo, hi))
-            if s < 2:
+        for i, block in enumerate(SPREAD + [TURNED]):
+            pick = sb.tile([P, P], F32, name=f"picked{i}", align_bytes=64)
+            looked_up = stat_table[:].indirect(entries(block))
+            if i < BLOCKS // 2:
                 nc.vector.tensor_copy(pick[:], looked_up)
             else:
                 nc.scalar.activation(pick[:], looked_up, COPY)
             picked.append(pick)
 
-        x_codes = shared.tile([P, S], U32, name="x_codes", align_bytes=64, offset=4 * T)
+        x_codes = sb.tile([P, S], U32, name="x_codes", align_bytes=64)
         nc.vector.tensor_copy(x_codes[:], word_table[:].bitcast(U32).indirect(offsets[:]))
 
-        means, neg_inv, neg_prod = [], [], []
-        for s, (lo, hi) in enumerate(STAT_PIECES):
-            blocks = (hi - lo) // P
-            turn = ps.tile([P, blocks, P], F32, name=f"turned{s}", tag=f"turned{s}")
-            for c in range(blocks):
-                nc.tensor.transpose(turn[:, c, :], picked[s][:, c * P : (c + 1) * P], identity[:])
-            if s == BLOCKS - 1:
-                first = sb.tile([P, 2], F32, name="first")
-                nc.scalar.activation(first[:], turn[:, 0, MEAN_ROW:], COPY)
-                last_mean = turn[:, 0, MEAN_ROW : MEAN_ROW + 1]
-                continue
-            column = sb.tile([P, blocks], F32, name=f"neg_inv{s}")
-            nc.scalar.activation(column[:], turn[:, :, INV_ROW], COPY, scale=-1.0)
-            for c in range(blocks):
-                means.append(turn[:, c, MEAN_ROW : MEAN_ROW + 1])
-                neg_inv.append(column[:, c : c + 1])
-        for c in range(BLOCKS - 1):
-            prod = sb.tile([P, 1], F32, name=f"neg_prod{c}")
-            nc.scalar.activation(prod[:], means[c], COPY, scale=neg_inv[c])
-            neg_prod.append(prod[:])
+        mean_cols, neg_invs, neg_prods = [], [], []
+        for i in range(BLOCKS):
+            turned = ps.tile([P, P], F32, name=f"turned{i}", tag=f"turned{i}")
+            nc.tensor.transpose(turned[:], picked[i][:], identity[:])
+            neg_inv = sb.tile([P, 1], F32, name=f"neg_inv{i}")
+            nc.scalar.activation(neg_inv[:], turned[:, INV_ROW : INV_ROW + 1], COPY, scale=-1.0)
+            mean_cols.append(turned[:, MEAN_ROW : MEAN_ROW + 1])
+            neg_invs.append(neg_inv[:])
+        for i in range(BLOCKS):
+            neg_prod = sb.tile([P, 1], F32, name=f"neg_prod{i}")
+            nc.scalar.activation(neg_prod[:], mean_cols[i], COPY, scale=neg_invs[i])
+            neg_prods.append(neg_prod[:])
 
-        first_prod = sb.tile([P, 1], F32, name="first_prod")
-        nc.scalar.activation(first_prod[:], last_mean, COPY, scale=first[:, 1:2])
-
-        def spread(name, columns, bank=None):
-            rows_ps = ps.tile([P, len(columns) * P], F32, name=name, tag=bank or name)
+        def spread(name, columns, bank):
+            rows_ps = ps.tile([P, len(columns) * P], F32, name=name, tag=bank)
             for c, column in enumerate(columns):
                 nc.tensor.transpose(rows_ps[:, c * P : (c + 1) * P], column.to_broadcast([P, P]), identity[:])
             return rows_ps
 
-        inv_ps = spread("inv_ps", neg_inv)
-        inv_rows = sb.tile([P, SPREAD], F32, name="inv_rows", align_bytes=64)
-        nc.scalar.activation(inv_rows[:], inv_ps[:], COPY, scale=-1.0)
+        inv_ps = spread("inv_ps", neg_invs[:-1], "inv_ps")
+        inv_rows = sb.tile([P, len(SPREAD), P], F32, name="inv_rows", align_bytes=64)
+        nc.scalar.activation(inv_rows[:].rearrange("p i j -> p (i j)"), inv_ps[:], COPY, scale=-1.0)
         gsum_ps = spread("gsum_ps", [gsum_col[:]], "turned2")
         neg_gsum_rows = sb.tile([P, N], F32, name="neg_gsum_rows", align_bytes=64)
         nc.scalar.activation(neg_gsum_rows[:], gsum_ps[:], COPY, scale=-1.0)
-        prod_ps = spread("prod_ps", neg_prod)
-        shift_rows = sb.tile([P, SPREAD], F32, name="shift_rows", align_bytes=64)
-        nc.scalar.activation(shift_rows[:], prod_ps[:], IDENTITY, bias=bias_col[:], scale=gsum_col[:])
+        prod_ps = spread("prod_ps", neg_prods[:-1], "prod_ps")
+        shift_rows = sb.tile([P, len(SPREAD), P], F32, name="shift_rows", align_bytes=64)
+        nc.scalar.activation(
+            shift_rows[:].rearrange("p i j -> p (i j)"), prod_ps[:], IDENTITY, bias=bias_col[:], scale=gsum_col[:]
+        )
         term = sb.tile([P, N], F32, name="term", align_bytes=64)
-        nc.scalar.activation(term[:], neg_gsum_rows[:], COPY, scale=first_prod[:])
+        nc.scalar.activation(term[:], neg_gsum_rows[:], COPY, scale=neg_prods[-1])
 
         w_codes = shared.tile([P, N], U32, name="w_codes", align_bytes=64, offset=S)
         w_scale = sb.tile([P, N], U8, name="w_scale", align_bytes=64)
+        weights = (w_codes[:].bitcast(FP8X4), w_scale[:])
 
-        sums = []
-        for n in range(BLOCKS):
-            lo, hi = ORDER[n] * P, (ORDER[n] + 1) * P
-            x_scale = shared.tile([P, P], U8, name=f"x_scale{n}", align_bytes=64, offset=(6 * T if n else 0) + lo)
-            nc.vector.tensor_copy(x_scale[:], scale_table[:].indirect(entries(lo, hi)))
-            if n == 0:
-                nc.vector.quantize_mx(
-                    out=w_codes[:].bitcast(FP8X4), scales=w_scale[:], in_=w_grouped[:].rearrange("p n j -> p (n j)")
-                )
-            acc = ps.tile([P, P], F32, name=f"acc{n}", tag=SUM_BANKS[n])
-            tokens = (x_codes[:, lo:hi].bitcast(FP8X4), x_scale[:])
-            weights = (w_codes[:].bitcast(FP8X4), w_scale[:])
-            still, moving = (weights, tokens) if n else (tokens, weights)
+        def gather_scales(block, count, offset):
+            x_scale = shared.tile([P, count * P], U8, name=f"x_scale{block}", align_bytes=64, offset=offset)
+            nc.vector.tensor_copy(x_scale[:], scale_table[:].indirect(entries(block, count)))
+            return x_scale
+
+        def product(block, scales, bank):
+            tokens = (x_codes[:, block * P : (block + 1) * P].bitcast(FP8X4), scales)
+            still, moving = (tokens, weights) if block == TURNED else (weights, tokens)
+            acc = ps.tile([P, P], F32, name=f"acc{block}", tag=bank)
             nc.tensor.matmul_mx(
                 out=acc[:],
                 lhsT=still[0],
@@ -157,31 +144,40 @@ def tile_picked_lnfold_none_p_kernel(
                 start=True,
                 stop=True,
             )
-            sums.append(acc)
-            if n == 0:
-                scaled_first = sb.tile([P, N], F32, name="scaled_first", align_bytes=64)
-                nc.scalar.activation(scaled_first[:], acc[:], COPY, scale=first[:, 1:2])
+            return acc
 
+        pair_scales = gather_scales(TURNED, 2, 0)
+        nc.vector.quantize_mx(
+            out=w_codes[:].bitcast(FP8X4), scales=w_scale[:], in_=w_grouped[:].rearrange("p n j -> p (n j)")
+        )
+        sums = [product(SPREAD[0], pair_scales[:, P:], "turned3")]
+        turned_sum = product(TURNED, pair_scales[:, 0:P], "turned0")
+        for i, bank in ((1, "turned1"), (2, "last_sum")):
+            sums.append(product(SPREAD[i], gather_scales(SPREAD[i], 1, 6 * T + i * P)[:], bank))
+
+        neg_scaled = sb.tile([P, N], F32, name="neg_scaled", align_bytes=64)
+        nc.scalar.activation(neg_scaled[:], turned_sum[:], COPY, scale=neg_invs[-1])
         back = ps.tile([P, P], F32, name="back", tag="back")
         nc.tensor.matmul(back[:], term[:], identity[:], start=True, stop=False, is_transpose=True)
-        nc.tensor.matmul(back[:], scaled_first[:], identity[:], start=False, stop=True, is_transpose=True)
+        nc.tensor.matmul(back[:], neg_scaled[:], identity[:], start=False, stop=True, is_transpose=True)
         result_pair = sb.tile([P, 2 * P], F32, name="result_pair", align_bytes=64)
-        nc.scalar.activation(result_pair[:, P:], back[:], IDENTITY, bias=bias_col[:])
+        nc.scalar.activation(result_pair[:, P:], back[:], IDENTITY, bias=bias_col[:], scale=-1.0)
 
-        def scale_piece(n):
-            scaled = sb.tile([P, P], F32, name=f"scaled{n}", align_bytes=64)
-            nc.vector.tensor_tensor(scaled[:], sums[n][:], inv_rows[:, ORDER[n] * P : (ORDER[n] + 1) * P], MULT)
+        def scale_block(i):
+            scaled = sb.tile([P, P], F32, name=f"scaled{i}", align_bytes=64)
+            nc.vector.tensor_tensor(scaled[:], sums[i][:], inv_rows[:, i, :], MULT)
             return scaled
 
-        def shift_and_store(n, scaled):
-            lo = ORDER[n] * P
-            result = result_pair if n == 2 else sb.tile([P, P], F32, name=f"result{n}", align_bytes=64)
-            nc.vector.tensor_tensor(result[:, 0:P], scaled[:], shift_rows[:, lo : lo + P], ADD)
+        def shift_and_store(i, scaled):
+            lo = SPREAD[i] * P
+            paired = SPREAD[i] + 1 == TURNED
+            result = result_pair if paired else sb.tile([P, P], F32, name=f"result{i}", align_bytes=64)
+            nc.vector.tensor_tensor(result[:, 0:P], scaled[:], shift_rows[:, i, :], ADD)
             nc.sync.dma_start(out=out[:, lo : lo + result.shape[1]], in_=result[:])
 
-        waiting = scale_piece(1)
-        for n in range(2, BLOCKS):
-            ahead = scale_piece(n)
-            shift_and_store(n - 1, waiting)
+        waiting = scale_block(0)
+        for i in range(1, len(SPREAD)):
+            ahead = scale_block(i)
+            shift_and_store(i - 1, waiting)
             waiting = ahead
-        shift_and_store(BLOCKS - 1, waiting)
+        shift_and_store(len(SPREAD) - 1, waiting)

@@ -25,7 +25,7 @@ GROUP = 16
 BLOCKS = S // P
 MEAN_ROW, INV_ROW = P - 2, P - 1
 TURNED = 2
-SPREAD = [3, 1, 0]
+SPREAD = [3, 0, 1]
 CLEARED = 8
 
 

@@ -93,14 +93,20 @@ def tile_picked_lnfold_none_p_kernel(
         for i in range(BLOCKS):
             turned = ps.tile([P, P], F32, name=f"turned{i}", tag=f"turned{i}")
             nc.tensor.transpose(turned[:], picked[i][:], identity[:])
+            if i == BLOCKS - 1:
+                turned_negated = sb.tile([P, 2], F32, name="turned_negated")
+                nc.scalar.activation(turned_negated[:], turned[:, MEAN_ROW:], COPY, scale=-1.0)
+                continue
             neg_inv = sb.tile([P, 1], F32, name=f"neg_inv{i}")
             nc.scalar.activation(neg_inv[:], turned[:, INV_ROW : INV_ROW + 1], COPY, scale=-1.0)
             mean_cols.append(turned[:, MEAN_ROW : MEAN_ROW + 1])
             neg_invs.append(neg_inv[:])
-        for i in range(BLOCKS):
+        for i in range(len(SPREAD)):
             neg_prod = sb.tile([P, 1], F32, name=f"neg_prod{i}")
             nc.scalar.activation(neg_prod[:], mean_cols[i], COPY, scale=neg_invs[i])
             neg_prods.append(neg_prod[:])
+        turned_prod = sb.tile([P, 1], F32, name="turned_prod")
+        nc.scalar.activation(turned_prod[:], turned_negated[:, 0:1], COPY, scale=turned_negated[:, 1:2])
 
         def spread(name, columns, bank):
             rows_ps = ps.tile([P, len(columns) * P], F32, name=name, tag=bank)
@@ -108,19 +114,17 @@ def tile_picked_lnfold_none_p_kernel(
                 nc.tensor.transpose(rows_ps[:, c * P : (c + 1) * P], column.to_broadcast([P, P]), identity[:])
             return rows_ps
 
-        inv_ps = spread("inv_ps", neg_invs[:-1], "inv_ps")
+        inv_ps = spread("inv_ps", neg_invs, "inv_ps")
         inv_rows = sb.tile([P, len(SPREAD), P], F32, name="inv_rows", align_bytes=64)
         nc.scalar.activation(inv_rows[:].rearrange("p i j -> p (i j)"), inv_ps[:], COPY, scale=-1.0)
         gsum_ps = spread("gsum_ps", [gsum_col[:]], "turned2")
-        neg_gsum_rows = sb.tile([P, N], F32, name="neg_gsum_rows", align_bytes=64)
-        nc.scalar.activation(neg_gsum_rows[:], gsum_ps[:], COPY, scale=-1.0)
-        prod_ps = spread("prod_ps", neg_prods[:-1], "prod_ps")
+        term = sb.tile([P, N], F32, name="term", align_bytes=64)
+        nc.scalar.activation(term[:], gsum_ps[:], COPY, scale=turned_prod[:])
+        prod_ps = spread("prod_ps", neg_prods, "prod_ps")
         shift_rows = sb.tile([P, len(SPREAD), P], F32, name="shift_rows", align_bytes=64)
         nc.scalar.activation(
             shift_rows[:].rearrange("p i j -> p (i j)"), prod_ps[:], IDENTITY, bias=bias_col[:], scale=gsum_col[:]
         )
-        term = sb.tile([P, N], F32, name="term", align_bytes=64)
-        nc.scalar.activation(term[:], neg_gsum_rows[:], COPY, scale=neg_prods[-1])
 
         w_codes = shared.tile([P, N], U32, name="w_codes", align_bytes=64, offset=S)
         w_scale = sb.tile([P, N], U8, name="w_scale", align_bytes=64)
@@ -150,13 +154,13 @@ def tile_picked_lnfold_none_p_kernel(
         nc.vector.quantize_mx(
             out=w_codes[:].bitcast(FP8X4), scales=w_scale[:], in_=w_grouped[:].rearrange("p n j -> p (n j)")
         )
-        sums = [product(SPREAD[0], pair_scales[:, P:], "turned3")]
-        turned_sum = product(TURNED, pair_scales[:, 0:P], "turned0")
+        turned_sum = product(TURNED, pair_scales[:, 0:P], "turned3")
+        sums = [product(SPREAD[0], pair_scales[:, P:], "turned0")]
         for i, bank in ((1, "turned1"), (2, "last_sum")):
             sums.append(product(SPREAD[i], gather_scales(SPREAD[i], 1, 6 * T + i * P)[:], bank))
 
         neg_scaled = sb.tile([P, N], F32, name="neg_scaled", align_bytes=64)
-        nc.scalar.activation(neg_scaled[:], turned_sum[:], COPY, scale=neg_invs[-1])
+        nc.scalar.activation(neg_scaled[:], turned_sum[:], COPY, scale=turned_negated[:, 1:2])
         back = ps.tile([P, P], F32, name="back", tag="back")
         nc.tensor.matmul(back[:], term[:], identity[:], start=True, stop=False, is_transpose=True)
         nc.tensor.matmul(back[:], neg_scaled[:], identity[:], start=False, stop=True, is_transpose=True)

from contextlib import ExitStack

import concourse.mybir as mybir
from concourse.masks import make_identity

K, T, S, N = 512, 1024, 512, 128
FLOPS = 2 * K * S * N

F32 = mybir.dt.float32
BF16 = mybir.dt.bfloat16
I32 = mybir.dt.int32
U32 = mybir.dt.uint32
U16 = mybir.dt.uint16
U8 = mybir.dt.uint8
FP8X4 = mybir.dt.float8_e4m3fn_x4
MULT = mybir.AluOpType.mult
ADD = mybir.AluOpType.add
COPY = mybir.ActivationFunctionType.Copy
IDENTITY = mybir.ActivationFunctionType.Identity

P = 128
PACK = 4
QUADRANT = 32
GROUP = 16
BLOCKS = S // P
MEAN_ROW, INV_ROW = P - 2, P - 1
TURNED = 2
SPREAD = [3, 0, 1]
CLEARED = 8


def tile_picked_lnfold_none_p_kernel(
    tc, x_words, x_scales, mean, inv, gsum, b, w1, offs, out
):
    nc = tc.nc
    with ExitStack() as ctx:
        sb = ctx.enter_context(tc.tile_pool(name="sb", bufs=1))
        shared = ctx.enter_context(tc.tile_pool(name="shared", bufs=1))
        ps = ctx.enter_context(tc.psum_pool(name="ps", bufs=1))

        offsets = sb.tile([P, S // GROUP], U16, name="offsets")
        nc.sync.dma_start(offsets[:], offs)

        def entries(block, count=1):
            return offsets[:, block * P // GROUP : (block + count) * P // GROUP]

        stat_table = shared.tile([P, T], F32, name="stat_table", align_bytes=64, offset=0)
        nc.scalar.dma_start(out=stat_table[INV_ROW : INV_ROW + 1, :], in_=inv[0:1, :])
        nc.sync.dma_start(out=stat_table[MEAN_ROW : MEAN_ROW + 1, :], in_=mean[0:1, :])
        scale_table = sb.tile([P, T], U8, name="scale_table", align_bytes=64)
        nc.vector.memset(scale_table[:].bitcast(I32), 0)
        nc.vector.memset(stat_table[0:MEAN_ROW, :], 0.0)

        word_table = sb.tile([P, T], I32, name="word_table", align_bytes=64)
        nc.sync.dma_start(out=word_table[:], in_=x_words[0].rearrange("p n t -> p (n t)").bitcast(I32))
        w_raw = shared.tile([P, PACK, N], F32, name="w_raw", align_bytes=64, offset=6 * T)
        nc.sync.dma_start(out=w_raw[:], in_=w1.rearrange("(p j) n -> p j n", j=PACK))

        for q in range(P // QUADRANT):
            nc.sync.dma_start(
                out=scale_table[QUADRANT * q : QUADRANT * q + PACK, :].bitcast(I32),
                in_=x_scales[0, PACK * q : PACK * (q + 1), :].bitcast(I32),
            )

        gsum_col = sb.tile([P, 1], F32, name="gsum_col")
        bias_col = sb.tile([P, 1], F32, name="bias_col")
        with nc.allow_non_contiguous_dma(reason="one value a partition"):
            nc.sync.dma_start(out=gsum_col[:], in_=gsum)
            nc.sync.dma_start(out=bias_col[:], in_=b)

        identity = sb.tile([P, P], F32, name="identity", align_bytes=64)
        nc.gpsimd.memset(identity[:, CLEARED:], 0.0)
        nc.scalar.activation(identity[:, 0:CLEARED], identity[:, CLEARED : 2 * CLEARED], COPY)
        make_identity(nc, identity[:], nomemset=True)

        w_grouped = sb.tile([P, N, PACK], BF16, name="w_grouped", align_bytes=64)
        nc.gpsimd.tensor_copy(w_grouped[:], w_raw[:].rearrange("p j n -> p n j"))

        picked = []
        for i, block in enumerate(SPREAD + [TURNED]):
            pick = sb.tile([P, P], F32, name=f"picked{i}", align_bytes=64)
            looked_up = stat_table[:].indirect(entries(block))
            if i < BLOCKS // 2:
                nc.vector.tensor_copy(pick[:], looked_up)
            else:
                nc.scalar.activation(pick[:], looked_up, COPY)
            picked.append(pick)

        x_codes = sb.tile([P, S], U32, name="x_codes", align_bytes=64)
        nc.vector.tensor_copy(x_codes[:], word_table[:].bitcast(U32).indirect(offsets[:]))

        mean_cols, neg_invs, neg_prods = [], [], []
        for i in range(BLOCKS):
            turned = ps.tile([P, P], F32, name=f"turned{i}", tag=f"turned{i}")
            nc.tensor.transpose(turned[:], picked[i][:], identity[:])
            if i == BLOCKS - 1:
                turned_negated = sb.tile([P, 2], F32, name="turned_negated")
                nc.scalar.activation(turned_negated[:], turned[:, MEAN_ROW:], COPY, scale=-1.0)
                continue
            neg_inv = sb.tile([P, 1], F32, name=f"neg_inv{i}")
            nc.scalar.activation(neg_inv[:], turned[:, INV_ROW : INV_ROW + 1], COPY, scale=-1.0)
            mean_cols.append(turned[:, MEAN_ROW : MEAN_ROW + 1])
            neg_invs.append(neg_inv[:])
        for i in range(len(SPREAD)):
            neg_prod = sb.tile([P, 1], F32, name=f"neg_prod{i}")
            nc.scalar.activation(neg_prod[:], mean_cols[i], COPY, scale=neg_invs[i])
            neg_prods.append(neg_prod[:])
        turned_prod = sb.tile([P, 1], F32, name="turned_prod")
        nc.scalar.activation(turned_prod[:], turned_negated[:, 0:1], COPY, scale=turned_negated[:, 1:2])

        def spread(name, columns, bank):
            rows_ps = ps.tile([P, len(columns) * P], F32, name=name, tag=bank)
            for c, column in enumerate(columns):
                nc.tensor.transpose(rows_ps[:, c * P : (c + 1) * P], column.to_broadcast([P, P]), identity[:])
            return rows_ps

        inv_ps = spread("inv_ps", neg_invs, "inv_ps")
        inv_rows = sb.tile([P, len(SPREAD), P], F32, name="inv_rows", align_bytes=64)
        nc.scalar.activation(inv_rows[:].rearrange("p i j -> p (i j)"), inv_ps[:], COPY, scale=-1.0)
        gsum_ps = spread("gsum_ps", [gsum_col[:]], "turned2")
        term = sb.tile([P, N], F32, name="term", align_bytes=64)
        nc.scalar.activation(term[:], gsum_ps[:], COPY, scale=turned_prod[:])
        prod_ps = spread("prod_ps", neg_prods, "prod_ps")
        shift_rows = sb.tile([P, len(SPREAD), P], F32, name="shift_rows", align_bytes=64)
        nc.scalar.activation(
            shift_rows[:].rearrange("p i j -> p (i j)"), prod_ps[:], IDENTITY, bias=bias_col[:], scale=gsum_col[:]
        )

        w_codes = shared.tile([P, N], U32, name="w_codes", align_bytes=64, offset=S)
        w_scale = sb.tile([P, N], U8, name="w_scale", align_bytes=64)
        weights = (w_codes[:].bitcast(FP8X4), w_scale[:])

        def gather_scales(block, count, offset):
            x_scale = shared.tile([P, count * P], U8, name=f"x_scale{block}", align_bytes=64, offset=offset)
            nc.vector.tensor_copy(x_scale[:], scale_table[:].indirect(entries(block, count)))
            return x_scale

        def product(block, scales, bank):
            tokens = (x_codes[:, block * P : (block + 1) * P].bitcast(FP8X4), scales)
            still, moving = (tokens, weights) if block == TURNED else (weights, tokens)
            acc = ps.tile([P, P], F32, name=f"acc{block}", tag=bank)
            nc.tensor.matmul_mx(
                out=acc[:],
                lhsT=still[0],
                lhsT_scale=still[1],
                rhs=moving[0],
                rhs_scale=moving[1],
                start=True,
                stop=True,
            )
            return acc

        pair_scales = gather_scales(TURNED, 2, 0)
        nc.vector.quantize_mx(
            out=w_codes[:].bitcast(FP8X4), scales=w_scale[:], in_=w_grouped[:].rearrange("p n j -> p (n j)")
        )
        turned_sum = product(TURNED, pair_scales[:, 0:P], "turned3")
        sums = [product(SPREAD[0], pair_scales[:, P:], "turned0")]
        for i, bank in ((1, "turned1"), (2, "last_sum")):
            sums.append(product(SPREAD[i], gather_scales(SPREAD[i], 1, 6 * T + i * P)[:], bank))

        neg_scaled = sb.tile([P, N], F32, name="neg_scaled", align_bytes=64)
        nc.scalar.activation(neg_scaled[:], turned_sum[:], COPY, scale=turned_negated[:, 1:2])
        back = ps.tile([P, P], F32, name="back", tag="back")
        nc.tensor.matmul(back[:], term[:], identity[:], start=True, stop=False, is_transpose=True)
        nc.tensor.matmul(back[:], neg_scaled[:], identity[:], start=False, stop=True, is_transpose=True)
        result_pair = sb.tile([P, 2 * P], F32, name="result_pair", align_bytes=64)
        nc.scalar.activation(result_pair[:, P:], back[:], IDENTITY, bias=bias_col[:], scale=-1.0)

        def scale_block(i):
            scaled = sb.tile([P, P], F32, name=f"scaled{i}", align_bytes=64)
            nc.vector.tensor_tensor(scaled[:], sums[i][:], inv_rows[:, i, :], MULT)
            return scaled

        def shift_and_store(i, scaled):
            lo = SPREAD[i] * P
            paired = SPREAD[i] + 1 == TURNED
            result = result_pair if paired else sb.tile([P, P], F32, name=f"result{i}", align_bytes=64)
            nc.vector.tensor_tensor(result[:, 0:P], scaled[:], shift_rows[:, i, :], ADD)
            nc.sync.dma_start(out=out[:, lo : lo + result.shape[1]], in_=result[:])

        waiting = scale_block(0)
        for i in range(1, len(SPREAD)):
            ahead = scale_block(i)
            shift_and_store(i - 1, waiting)
            waiting = ahead
        shift_and_store(len(SPREAD) - 1, waiting)
